import numpy as np
import ml_dtypes


def mxq(x, axis, fmt="e4m3"):
    dtype, down = {"e4m3": (ml_dtypes.float8_e4m3fn, 7), "e5m2": (ml_dtypes.float8_e5m2, 14)}[fmt]
    v = np.moveaxis(np.asarray(x, np.float32).astype(ml_dtypes.bfloat16).astype(np.float64), axis, -1)
    blocks = v.reshape(v.shape[:-1] + (-1, 32))
    amax = np.abs(blocks).max(-1, keepdims=True)
    byte = np.maximum(np.where(amax > 0, np.frexp(amax)[1] - 1 + 127, 0) - down, 1)
    scale = np.exp2(byte - 127.0)
    codes = (blocks / scale).astype(np.float32).astype(dtype).astype(np.float64)
    return np.moveaxis((codes * scale).reshape(v.shape), -1, axis)


WIDE = False


def mx_kscale(k):
    if not WIDE:
        return np.ones(k)
    levels = np.array([10, -10, 5, -5, 0])
    if k % 512:
        return np.exp2(np.random.permutation(np.resize(levels, k // 32))).repeat(32)
    a = np.empty((k // 512, 16))
    for p in range(k // 512):
        a[p, :8] = np.random.permutation(np.resize(levels, 8))
        for g in range(8):
            far = levels[np.abs(levels - a[p, g]) >= 10]
            a[p, g + 8] = far[np.random.randint(len(far))]
    return np.exp2(a.ravel()).repeat(32)


def f64(x):
    return np.asarray(x).astype(np.float64)


def striped(idx):
    return np.tile(idx.reshape(-1, 16).T, (8, 1)).astype(np.uint16)


def unstriped(offs):
    return offs[:16].T.reshape(-1).astype(np.int64)


def relu(v):
    return np.maximum(v, 0.0)


def d_relu(v):
    return (v > 0).astype(np.float64)


K, T, E, C, H, N = 128, 512, 8, 256, 512, 1536
TOP = 4


def by_expert(wq, xq):
    return np.concatenate([wq[e].T @ xq[:, e * C:(e + 1) * C] for e in range(E)], axis=1)


def setup_inputs():
    n = np.random.standard_normal
    s = mx_kscale(N)[:, None]
    u = mx_kscale(H)
    deal = np.repeat(np.arange(E), C).reshape(TOP, T)[:, np.random.permutation(T)]
    deal = np.take_along_axis(deal, np.argsort(np.random.rand(TOP, T), axis=0), axis=0)
    for _ in range(8):
        s_, t_ = np.random.permutation(T).reshape(2, -1); r = np.random.randint(TOP, size=T // 2); x, y = deal[r, s_].copy(), deal[r, t_].copy()
        ok = ~((deal[:, s_] == y).any(0) | (deal[:, t_] == x).any(0)); deal[r[ok], s_[ok]] = y[ok]; deal[r[ok], t_[ok]] = x[ok]
    order = np.lexsort((np.random.rand(TOP * T), deal.reshape(-1)))
    slot_token = order % T; pos = np.empty(TOP * T, np.int64); pos[order] = np.arange(TOP * T); pos = pos.reshape(TOP, T)
    g = np.random.uniform(0.5, 1.5, (TOP, T)); g = g / g.sum(0)
    w_slot = np.empty(E * C)
    for r in range(TOP): w_slot[pos[r]] = g[r]
    return {
        "dyT": (n((N, T)) * s).astype(np.float32),
        "a1": n((H, E * C)).astype(np.float32),
        "a3": n((H, E * C)).astype(np.float32),
        "w2": (n((E, N, H)) / np.sqrt(N) / s[None] * u[None, None, :]).astype(np.float32),
        "w1": (n((E, H, K)) / np.sqrt(H) / u[None, :, None]).astype(np.float32),
        "w3": (n((E, H, K)) / np.sqrt(H) / u[None, :, None]).astype(np.float32),
        "gate": np.tile(w_slot, (N, 1)).astype(np.float32),
        "offs": striped(slot_token),
        "pos1": striped(pos[0]),
        "pos2": striped(pos[1]),
        "pos3": striped(pos[2]),
        "pos4": striped(pos[3]),
    }


def reference(dyT, a1, a3, w2, w1, w3, gate, offs, pos1, pos2, pos3, pos4):
    idx = unstriped(offs)
    gq = mxq(f64(gate) * f64(dyT)[:, idx], 0, "e4m3")
    dh = by_expert(mxq(f64(w2), 1, "e4m3"), gq)
    da1 = dh * f64(a3) * d_relu(f64(a1))
    da3 = dh * relu(f64(a1))
    dx = by_expert(mxq(f64(w1), 1, "e4m3"), mxq(da1, 0, "e4m3")) + by_expert(mxq(f64(w3), 1, "e4m3"), mxq(da3, 0, "e4m3"))
    return dx[:, unstriped(pos1)] + dx[:, unstriped(pos2)] + dx[:, unstriped(pos3)] + dx[:, unstriped(pos4)]

@@ -1,0 +1,230 @@
+from contextlib import ExitStack
+
+import concourse.mybir as mybir
+
+K, T, E, C, H, N = 128, 512, 8, 256, 512, 1536
+S = E * C
+P = 128
+PACK = 4
+K_PASS = P * PACK
+PASSES = N // K_PASS
+PAIR = 2
+GROUPS = E // PAIR
+GS = PAIR * C
+SPARE = 16
+PER_COL = 16
+
+FLOPS = 2 * S * (N * H + 2 * H * K)
+BYTES = 4 * (N * T + 2 * H * S + E * N * H + 2 * E * H * K + S + K * T) + 2 * P * (S + 4 * T) // PER_COL
+
+F32 = mybir.dt.float32
+BF16 = mybir.dt.bfloat16
+U32 = mybir.dt.uint32
+U16 = mybir.dt.uint16
+U8 = mybir.dt.uint8
+FP8X4 = mybir.dt.float8_e4m3fn_x4
+ALU = mybir.AluOpType
+
+
+def tile_moe_bdx_glu_relu_kernel(
+    tc, dyT, a1, a3, w2, w1, w3, gate, offs, pos1, pos2, pos3, pos4, out
+):
+    nc = tc.nc
+    with ExitStack() as ctx:
+        keep = ctx.enter_context(tc.tile_pool(name="keep", bufs=1))
+        ring = ctx.enter_context(tc.tile_pool(name="ring", bufs=2))
+        psum = ctx.enter_context(tc.psum_pool(name="psum", bufs=1))
+
+        offs_sb = keep.tile([P, S // PER_COL], U16, name="offs_sb")
+        pos_sb = [keep.tile([P, T // PER_COL], U16, name="pos_sb%d" % r) for r in range(4)]
+        gate_sb = [keep.tile([P, GS], F32, name="gate_sb%d" % g) for g in range(GROUPS)]
+        dy_sb = [keep.tile([P, T + SPARE], F32, name="dy_sb%d" % q) for q in range(PASSES * PACK)]
+        dx_sb = keep.tile([P, S], F32, name="dx_sb")
+
+        w2_raw, w2_bf, w2_mx = {}, {}, {}
+        g_raw, g_bf, g_mx = {}, {}, {}
+        w13_raw, w13_bf, w13_mx = {}, {}, {}
+        acts, dh, dhm, da_bf, da_mx, dx_ps = {}, {}, {}, {}, {}, {}
+
+        def quantize(name, src, bufs):
+            width = src.shape[1] // PACK
+            codes = ring.tile([P, width], U32, name=name + "_codes", bufs=bufs, align_bytes=64)
+            scales = ring.tile([P, width], U8, name=name + "_scales", bufs=bufs, align_bytes=64)
+            nc.vector.quantize_mx(out=codes[:].bitcast(FP8X4), scales=scales[:], in_=src)
+            return codes, scales
+
+        def load_gate(g):
+            nc.sync.dma_start(out=gate_sb[g][:], in_=gate[0:P, g * GS:(g + 1) * GS])
+
+        def load_dy(c):
+            rows = dyT[c * K_PASS:(c + 1) * K_PASS, :].rearrange("(p t) w -> p t w", t=PACK)
+            for t in range(PACK):
+                nc.sync.dma_start(out=dy_sb[c * PACK + t][:, 0:T], in_=rows[:, t, :])
+
+        def load_w2(u):
+            e, c = divmod(u, PASSES)
+            w2_raw[u] = ring.tile([P, PACK, H], F32, name="w2_raw", bufs=4)
+            nc.sync.dma_start(
+                out=w2_raw[u][:],
+                in_=w2[e, c * K_PASS:(c + 1) * K_PASS, :].rearrange("(p j) i -> p j i", j=PACK),
+            )
+
+        def load_group(g):
+            w13_raw[g] = ring.tile([P, 2, PAIR, PACK * K], F32, name="w13_raw", bufs=1)
+            for m, w in enumerate((w1, w3)):
+                nc.sync.dma_start(
+                    out=w13_raw[g][:, m, :, :],
+                    in_=w[g * PAIR:(g + 1) * PAIR].rearrange("e (p j) k -> p e (j k)", j=PACK),
+                )
+            acts[g] = []
+            for m, a in enumerate((a1, a3)):
+                a_sb = ring.tile([P, PACK, GS], F32, name="a_sb%d" % m, bufs=2)
+                nc.sync.dma_start(
+                    out=a_sb[:], in_=a[:, g * GS:(g + 1) * GS].rearrange("(p t) s -> p t s", t=PACK)
+                )
+                acts[g].append(a_sb)
+
+        def gather(n):
+            g, c = divmod(n, PASSES)
+            g_raw[n] = ring.tile([P, PACK, GS], F32, name="g_raw", bufs=3)
+            cols = slice(g * GS // PER_COL, (g + 1) * GS // PER_COL)
+            for t in range(PACK):
+                nc.vector.tensor_tensor(
+                    g_raw[n][:, t, :], dy_sb[c * PACK + t][:].indirect(offs_sb[:, cols]), gate_sb[g][:], ALU.mult
+                )
+
+        def round_g(n):
+            g_bf[n] = ring.tile([P, GS * PACK], BF16, name="g_bf", bufs=3, align_bytes=64)
+            nc.scalar.copy(
+                out=g_bf[n][:].rearrange("p (a b t) -> p a t b", b=2, t=PACK),
+                in_=g_raw[n][:].rearrange("p t (a b) -> p a t b", b=2),
+            )
+
+        def round_w2(u):
+            w2_bf[u] = ring.tile([P, H * PACK], BF16, name="w2_bf", bufs=3, align_bytes=64)
+            nc.scalar.copy(
+                out=w2_bf[u][:].rearrange("p (th tl m j) -> p m th j tl", th=2, tl=2, j=PACK),
+                in_=w2_raw[u][:].rearrange("p j (m th tl) -> p m th j tl", th=2, tl=2),
+            )
+
+        def round_w13(g):
+            w13_bf[g] = ring.tile([P, 2 * PAIR * K * PACK], BF16, name="w13_bf", bufs=1, align_bytes=64)
+            nc.scalar.copy(
+                out=w13_bf[g][:].rearrange("p (x a b j) -> p x a j b", b=2, j=PACK, x=2 * PAIR),
+                in_=w13_raw[g][:].rearrange("p m e (j a b) -> p (m e) a j b", b=2, j=PACK),
+            )
+
+        def first_product(e):
+            g, half = divmod(e, PAIR)
+            slots = slice(half * C, (half + 1) * C)
+            dh[e] = [psum.tile([P, 2, C], F32, name="dh%d" % b, bufs=3) for b in range(2)]
+            for t in range(PACK):
+                cols = slice(t * P, (t + 1) * P)
+                for c in range(PASSES):
+                    w_codes, w_scales = w2_mx[e * PASSES + c]
+                    g_codes, g_scales = g_mx[g * PASSES + c]
+                    nc.tensor.matmul_mx(
+                        out=dh[e][t // 2][:, t % 2, :],
+                        lhsT=w_codes[:, cols].bitcast(FP8X4), lhsT_scale=w_scales[:, cols],
+                        rhs=g_codes[:, slots].bitcast(FP8X4), rhs_scale=g_scales[:, slots],
+                        start=(c == 0), stop=(c == PASSES - 1),
+                    )
+
+        def mask_dh(e):
+            g, half = divmod(e, PAIR)
+            slots = slice(half * C, (half + 1) * C)
+            dhm[e] = ring.tile([P, PACK, C], F32, name="dhm", bufs=2)
+            for b in range(2):
+                nc.vector.scalar_tensor_tensor(
+                    out=dhm[e][:, 2 * b:2 * b + 2, :], in0=acts[g][0][:, 2 * b:2 * b + 2, slots], scalar=0.0,
+                    in1=dh[e][b][:], op0=ALU.is_gt, op1=ALU.mult,
+                )
+
+        def make_da(e):
+            g, half = divmod(e, PAIR)
+            slots = slice(half * C, (half + 1) * C)
+            da_bf[e] = []
+            for m in range(2):
+                da = ring.tile([P, C * PACK], BF16, name="da_bf%d" % m, bufs=2, align_bytes=64)
+                nc.vector.tensor_tensor(
+                    da[:].rearrange("p (a b t) -> p a t b", b=2, t=PACK),
+                    dhm[e][:].rearrange("p t (a b) -> p a t b", b=2),
+                    acts[g][1 - m][:, :, slots].rearrange("p t (a b) -> p a t b", b=2),
+                    ALU.mult,
+                )
+                da_bf[e].append(da)
+
+        def second_product(e):
+            g, half = divmod(e, PAIR)
+            da_mx[e] = [quantize("da%d" % m, da_bf[e][m][:], 2) for m in range(2)]
+            dx_ps[e] = psum.tile([P, C], F32, name="dx_ps", bufs=2)
+            w_codes, w_scales = w13_mx[g]
+            for m in range(2):
+                cols = slice((m * PAIR + half) * K, (m * PAIR + half + 1) * K)
+                nc.tensor.matmul_mx(
+                    out=dx_ps[e][:],
+                    lhsT=w_codes[:, cols].bitcast(FP8X4), lhsT_scale=w_scales[:, cols],
+                    rhs=da_mx[e][m][0][:].bitcast(FP8X4), rhs_scale=da_mx[e][m][1][:],
+                    start=(m == 0), stop=(m == 1),
+                )
+            nc.scalar.copy(out=dx_sb[:, e * C:(e + 1) * C], in_=dx_ps[e][:])
+
+        steps = GROUPS * PASSES
+        for q in range(PASSES * PACK):
+            nc.gpsimd.memset(dy_sb[q][:, T:T + SPARE], 0.0)
+        nc.sync.dma_start(out=offs_sb[:], in_=offs)
+        load_gate(0)
+        for c in range(PASSES):
+            load_dy(c)
+            load_w2(c)
+        for n in range(steps + 3):
+            g, c = divmod(n, PASSES)
+            for u in (2 * n + 3, 2 * n + 4):
+                if u < E * PASSES:
+                    load_w2(u)
+            if c == 1 and g < GROUPS:
+                if g + 1 < GROUPS:
+                    load_gate(g + 1)
+                load_group(g)
+            if n == steps - PASSES:
+                for r, pos in enumerate((pos1, pos2, pos3, pos4)):
+                    nc.sync.dma_start(out=pos_sb[r][:], in_=pos)
+            if n < steps:
+                gather(n)
+                round_w2(2 * n)
+                round_g(n)
+                round_w2(2 * n + 1)
+                if c == 2:
+                    round_w13(g)
+            late = PAIR * (g - 1) + c - 1
+            if c >= 1 and late >= 0:
+                mask_dh(late)
+            if 1 <= n <= steps:
+                g_mx[n - 1] = quantize("g", g_bf[n - 1][:], 5)
+                if c == 0:
+                    first_product(PAIR * g - 2)
+            if c >= 1 and late >= 0:
+                make_da(late)
+            if 1 <= n <= steps:
+                for u in (2 * n - 2, 2 * n - 1):
+                    w2_mx[u] = quantize("w2", w2_bf[u][:], 8)
+                if c == 0:
+                    first_product(PAIR * g - 1)
+                    w13_mx[g - 1] = quantize("w13", w13_bf[g - 1][:], 2)
+            if c >= 1 and late >= 0:
+                second_product(late)
+
+        halves = 2
+        th = T // halves
+        acc = [None] * halves
+        for r in range(4):
+            for h in range(halves):
+                picked = dx_sb[:].indirect(pos_sb[r][:, h * th // PER_COL:(h + 1) * th // PER_COL])
+                total = keep.tile([P, th], F32, name="total%d_%d" % (r, h))
+                if r == 0:
+                    nc.vector.tensor_copy(total[:], picked)
+                else:
+                    nc.vector.tensor_tensor(total[:], picked, acc[h][:], ALU.add)
+                acc[h] = total
+        for h in range(halves):
+            nc.sync.dma_start(out=out[:, h * th:(h + 1) * th], in_=acc[h][:])

@@ -103,8 +103,8 @@ def tile_moe_bdx_glu_relu_kernel(
         def round_w2(u):
             w2_bf[u] = ring.tile([P, H * PACK], BF16, name="w2_bf", bufs=3, align_bytes=64)
             nc.scalar.copy(
-                out=w2_bf[u][:].rearrange("p (th tl m j) -> p m th j tl", th=2, tl=2, j=PACK),
-                in_=w2_raw[u][:].rearrange("p j (m th tl) -> p m th j tl", th=2, tl=2),
+                out=w2_bf[u][:].rearrange("p (th tl m j) -> p th m j tl", th=2, tl=2, j=PACK),
+                in_=w2_raw[u][:].rearrange("p j (m th tl) -> p th m j tl", th=2, tl=2),
             )
 
         def round_w13(g):

@@ -3,19 +3,33 @@ from contextlib import ExitStack
 import concourse.mybir as mybir
 
 K, T, E, C, H, N = 128, 512, 8, 256, 512, 1536
+TOP = 4
 S = E * C
+
 P = 128
 PACK = 4
 K_PASS = P * PACK
 PASSES = N // K_PASS
 PAIR = 2
-GROUPS = E // PAIR
-GS = PAIR * C
-SPARE = 16
+PAIRS = E // PAIR
+PAIR_SLOTS = PAIR * C
+STEPS = PAIRS * PASSES
+W2_TILES = E * PASSES
 PER_COL = 16
+SPARE = 16
+
+TILE_WORDS = PAIR_SLOTS * PACK // 2
+STRETCH = PAIR_SLOTS + C
+REGION_WORDS = TILE_WORDS + PACK * STRETCH
+W2_AT = TILE_WORDS - 16
+REGIONS = 4
+
+W2_QUANT_LAG = 2
+DA_LAG = 5
+DY_LEAD = 4
 
 FLOPS = 2 * S * (N * H + 2 * H * K)
-BYTES = 4 * (N * T + 2 * H * S + E * N * H + 2 * E * H * K + S + K * T) + 2 * P * (S + 4 * T) // PER_COL
+BYTES = 4 * (N * T + 2 * H * S + E * N * H + 2 * E * H * K + S + K * T) + 2 * P * (S + TOP * T) // PER_COL
 
 F32 = mybir.dt.float32
 BF16 = mybir.dt.bfloat16
@@ -36,15 +50,25 @@ def tile_moe_bdx_glu_relu_kernel(
         psum = ctx.enter_context(tc.psum_pool(name="psum", bufs=1))
 
         offs_sb = keep.tile([P, S // PER_COL], U16, name="offs_sb")
-        pos_sb = [keep.tile([P, T // PER_COL], U16, name="pos_sb%d" % r) for r in range(4)]
-        gate_sb = [keep.tile([P, GS], F32, name="gate_sb%d" % g) for g in range(GROUPS)]
+        pos_sb = [keep.tile([P, T // PER_COL], U16, name="pos_sb%d" % r) for r in range(TOP)]
+        gate_sb = [keep.tile([P, PAIR_SLOTS], F32, name="gate_sb%d" % g) for g in range(PAIRS)]
         dy_sb = [keep.tile([P, T + SPARE], F32, name="dy_sb%d" % q) for q in range(PASSES * PACK)]
         dx_sb = keep.tile([P, S], F32, name="dx_sb")
+        stage = [keep.tile([P, REGION_WORDS], F32, name="stage%d" % r, align_bytes=64) for r in range(REGIONS)]
 
-        w2_raw, w2_bf, w2_mx = {}, {}, {}
+        w2_raw, w2_mx = {}, {}
         g_raw, g_bf, g_mx = {}, {}, {}
         w13_raw, w13_bf, w13_mx = {}, {}, {}
-        acts, dh, dhm, da_bf, da_mx, dx_ps = {}, {}, {}, {}, {}, {}
+        saved, dh, dh_masked, da_bf = {}, {}, {}, {}
+
+        def w2_region(n):
+            return stage[n % REGIONS]
+
+        def second_use(n):
+            return w2_region(n - 1 - W2_QUANT_LAG)
+
+        def stretches(n):
+            return second_use(n)[:, TILE_WORDS:REGION_WORDS].rearrange("p (t s) -> p t s", t=PACK)
 
         def quantize(name, src, bufs):
             width = src.shape[1] // PACK
@@ -54,56 +78,59 @@ def tile_moe_bdx_glu_relu_kernel(
             return codes, scales
 
         def load_gate(g):
-            nc.sync.dma_start(out=gate_sb[g][:], in_=gate[0:P, g * GS:(g + 1) * GS])
+            nc.sync.dma_start(out=gate_sb[g][:], in_=gate[0:P, g * PAIR_SLOTS:(g + 1) * PAIR_SLOTS])
 
-        def load_dy(c):
+        def load_dy(q):
+            c, t = divmod(q, PACK)
             rows = dyT[c * K_PASS:(c + 1) * K_PASS, :].rearrange("(p t) w -> p t w", t=PACK)
-            for t in range(PACK):
-                nc.sync.dma_start(out=dy_sb[c * PACK + t][:, 0:T], in_=rows[:, t, :])
+            nc.sync.dma_start(out=dy_sb[q][:, 0:T], in_=rows[:, t, :])
 
-        def load_w2(u):
+        def load_w2(u, planes=slice(0, PACK)):
             e, c = divmod(u, PASSES)
-            w2_raw[u] = ring.tile([P, PACK, H], F32, name="w2_raw", bufs=4)
-            nc.sync.dma_start(
-                out=w2_raw[u][:],
-                in_=w2[e, c * K_PASS:(c + 1) * K_PASS, :].rearrange("(p j) i -> p j i", j=PACK),
-            )
+            if u not in w2_raw:
+                w2_raw[u] = ring.tile([P, PACK, H], F32, name="w2_raw", bufs=4)
+            rows = w2[e, c * K_PASS:(c + 1) * K_PASS, :].rearrange("(p j) i -> p j i", j=PACK)
+            nc.sync.dma_start(out=w2_raw[u][:, planes, :], in_=rows[:, planes, :])
 
-        def load_group(g):
+        def load_w13(g):
             w13_raw[g] = ring.tile([P, 2, PAIR, PACK * K], F32, name="w13_raw", bufs=1)
             for m, w in enumerate((w1, w3)):
                 nc.sync.dma_start(
                     out=w13_raw[g][:, m, :, :],
                     in_=w[g * PAIR:(g + 1) * PAIR].rearrange("e (p j) k -> p e (j k)", j=PACK),
                 )
-            acts[g] = []
+
+        def load_saved(e):
+            saved[e] = []
             for m, a in enumerate((a1, a3)):
-                a_sb = ring.tile([P, PACK, GS], F32, name="a_sb%d" % m, bufs=2)
-                nc.sync.dma_start(
-                    out=a_sb[:], in_=a[:, g * GS:(g + 1) * GS].rearrange("(p t) s -> p t s", t=PACK)
-                )
-                acts[g].append(a_sb)
+                a_sb = ring.tile([P, PACK, C], F32, name="a_sb%d_%d" % (m, e % PAIR), bufs=1)
+                nc.sync.dma_start(out=a_sb[:], in_=a[:, e * C:(e + 1) * C].rearrange("(p t) s -> p t s", t=PACK))
+                saved[e].append(a_sb)
 
         def gather(n):
             g, c = divmod(n, PASSES)
-            g_raw[n] = ring.tile([P, PACK, GS], F32, name="g_raw", bufs=3)
-            cols = slice(g * GS // PER_COL, (g + 1) * GS // PER_COL)
+            g_raw[n] = stretches(n)[:, :, 0:PAIR_SLOTS]
+            cols = slice(g * PAIR_SLOTS // PER_COL, (g + 1) * PAIR_SLOTS // PER_COL)
             for t in range(PACK):
                 nc.vector.tensor_tensor(
                     g_raw[n][:, t, :], dy_sb[c * PACK + t][:].indirect(offs_sb[:, cols]), gate_sb[g][:], ALU.mult
                 )
 
         def round_g(n):
-            g_bf[n] = ring.tile([P, GS * PACK], BF16, name="g_bf", bufs=3, align_bytes=64)
+            if n < STEPS - 1:
+                g_bf[n] = second_use(n + 1)[:, 0:TILE_WORDS].bitcast(BF16)
+            else:
+                g_bf[n] = keep.tile([P, PAIR_SLOTS * PACK], BF16, name="g_last", align_bytes=64)[:]
             nc.scalar.copy(
-                out=g_bf[n][:].rearrange("p (a b t) -> p a t b", b=2, t=PACK),
-                in_=g_raw[n][:].rearrange("p t (a b) -> p a t b", b=2),
+                out=g_bf[n].rearrange("p (a b t) -> p a t b", b=2, t=PACK),
+                in_=g_raw[n].rearrange("p t (a b) -> p a t b", b=2),
             )
 
         def round_w2(u):
-            w2_bf[u] = ring.tile([P, H * PACK], BF16, name="w2_bf", bufs=3, align_bytes=64)
+            first = W2_AT + TILE_WORDS * (u % 2)
+            rounded = w2_region(u // 2)[:, first:first + TILE_WORDS].bitcast(BF16)
             nc.scalar.copy(
-                out=w2_bf[u][:].rearrange("p (th tl m j) -> p th m j tl", th=2, tl=2, j=PACK),
+                out=rounded.rearrange("p (th tl m j) -> p th m j tl", th=2, tl=2, j=PACK),
                 in_=w2_raw[u][:].rearrange("p j (m th tl) -> p th m j tl", th=2, tl=2),
             )
 
@@ -118,113 +145,134 @@ def tile_moe_bdx_glu_relu_kernel(
             g, half = divmod(e, PAIR)
             slots = slice(half * C, (half + 1) * C)
             dh[e] = [psum.tile([P, 2, C], F32, name="dh%d" % b, bufs=3) for b in range(2)]
-            for t in range(PACK):
-                cols = slice(t * P, (t + 1) * P)
+            for t in (0, 2, 1, 3):
                 for c in range(PASSES):
-                    w_codes, w_scales = w2_mx[e * PASSES + c]
+                    step, second = divmod(e * PASSES + c, 2)
+                    w_codes, w_scales = w2_mx[step]
+                    cols = slice(second * H + t * P, second * H + (t + 1) * P)
                     g_codes, g_scales = g_mx[g * PASSES + c]
                     nc.tensor.matmul_mx(
-                        out=dh[e][t // 2][:, t % 2, :],
+                        out=dh[e][t % 2][:, t // 2, :],
                         lhsT=w_codes[:, cols].bitcast(FP8X4), lhsT_scale=w_scales[:, cols],
                         rhs=g_codes[:, slots].bitcast(FP8X4), rhs_scale=g_scales[:, slots],
                         start=(c == 0), stop=(c == PASSES - 1),
                     )
 
-        def mask_dh(e):
-            g, half = divmod(e, PAIR)
-            slots = slice(half * C, (half + 1) * C)
-            dhm[e] = ring.tile([P, PACK, C], F32, name="dhm", bufs=2)
+        def first_products_that_are_ready():
+            for e in range(E):
+                last_w2_step = (e * PASSES + PASSES - 1) // 2
+                last_g_step = (e // PAIR) * PASSES + PASSES - 1
+                if e not in dh and last_w2_step in w2_mx and last_g_step in g_mx:
+                    first_product(e)
+
+        def mask_dh(e, n):
+            dh_masked[e] = stretches(n)[:, :, PAIR_SLOTS:STRETCH]
             for b in range(2):
                 nc.vector.scalar_tensor_tensor(
-                    out=dhm[e][:, 2 * b:2 * b + 2, :], in0=acts[g][0][:, 2 * b:2 * b + 2, slots], scalar=0.0,
+                    out=dh_masked[e][:, b:PACK:2, :], in0=saved[e][0][:, b:PACK:2, :], scalar=0.0,
                     in1=dh[e][b][:], op0=ALU.is_gt, op1=ALU.mult,
                 )
 
         def make_da(e):
-            g, half = divmod(e, PAIR)
-            slots = slice(half * C, (half + 1) * C)
             da_bf[e] = []
             for m in range(2):
                 da = ring.tile([P, C * PACK], BF16, name="da_bf%d" % m, bufs=2, align_bytes=64)
                 nc.vector.tensor_tensor(
                     da[:].rearrange("p (a b t) -> p a t b", b=2, t=PACK),
-                    dhm[e][:].rearrange("p t (a b) -> p a t b", b=2),
-                    acts[g][1 - m][:, :, slots].rearrange("p t (a b) -> p a t b", b=2),
+                    dh_masked[e].rearrange("p t (a b) -> p a t b", b=2),
+                    saved[e][1 - m][:].rearrange("p t (a b) -> p a t b", b=2),
                     ALU.mult,
                 )
                 da_bf[e].append(da)
 
         def second_product(e):
             g, half = divmod(e, PAIR)
-            da_mx[e] = [quantize("da%d" % m, da_bf[e][m][:], 2) for m in range(2)]
-            dx_ps[e] = psum.tile([P, C], F32, name="dx_ps", bufs=2)
+            da_mx = [quantize("da%d" % m, da_bf[e][m][:], 2) for m in range(2)]
+            dx_ps = psum.tile([P, C], F32, name="dx_ps", bufs=2)
             w_codes, w_scales = w13_mx[g]
             for m in range(2):
                 cols = slice((m * PAIR + half) * K, (m * PAIR + half + 1) * K)
                 nc.tensor.matmul_mx(
-                    out=dx_ps[e][:],
+                    out=dx_ps[:],
                     lhsT=w_codes[:, cols].bitcast(FP8X4), lhsT_scale=w_scales[:, cols],
-                    rhs=da_mx[e][m][0][:].bitcast(FP8X4), rhs_scale=da_mx[e][m][1][:],
+                    rhs=da_mx[m][0][:].bitcast(FP8X4), rhs_scale=da_mx[m][1][:],
                     start=(m == 0), stop=(m == 1),
                 )
-            nc.scalar.copy(out=dx_sb[:, e * C:(e + 1) * C], in_=dx_ps[e][:])
+            nc.scalar.copy(out=dx_sb[:, e * C:(e + 1) * C], in_=dx_ps[:])
 
-        steps = GROUPS * PASSES
+        def pairs_whose_w13_was_loaded_in(n):
+            return [g for g in range(PAIRS) if n == PASSES * max(g - 1, 0)]
+
+        expert_of_step = {PASSES * (e // PAIR) + e % PAIR + DA_LAG: e for e in range(E)}
+
         for q in range(PASSES * PACK):
             nc.gpsimd.memset(dy_sb[q][:, T:T + SPARE], 0.0)
         nc.sync.dma_start(out=offs_sb[:], in_=offs)
         load_gate(0)
-        for c in range(PASSES):
-            load_dy(c)
-            load_w2(c)
-        for n in range(steps + 3):
+        for i in range(PASSES * PACK + DY_LEAD):
+            if i < PASSES * PACK:
+                load_dy(i)
+            if i >= DY_LEAD:
+                u, j = divmod(i - DY_LEAD, PACK)
+                load_w2(u, slice(j, j + 1))
+
+        for n in range(max(expert_of_step) + 1):
             g, c = divmod(n, PASSES)
-            for u in (2 * n + 3, 2 * n + 4):
-                if u < E * PASSES:
+            e = expert_of_step.get(n)
+
+            if c == 0 and g + 1 < PAIRS:
+                load_gate(g + 1)
+            for u in (PASSES + 2 * n, PASSES + 2 * n + 1):
+                if u < W2_TILES:
                     load_w2(u)
-            if c == 1 and g < GROUPS:
-                if g + 1 < GROUPS:
-                    load_gate(g + 1)
-                load_group(g)
-            if n == steps - PASSES:
+            for x in pairs_whose_w13_was_loaded_in(n):
+                load_w13(x)
+            if 1 <= n <= PAIR:
+                load_saved(n - 1)
+            if n == STEPS - PASSES:
                 for r, pos in enumerate((pos1, pos2, pos3, pos4)):
                     nc.sync.dma_start(out=pos_sb[r][:], in_=pos)
-            if n < steps:
+
+            if n < STEPS:
                 gather(n)
+                if n >= 1:
+                    round_g(n - 1)
+                if n == STEPS - 1:
+                    round_g(n)
                 round_w2(2 * n)
-                round_g(n)
                 round_w2(2 * n + 1)
-                if c == 2:
-                    round_w13(g)
-            late = PAIR * (g - 1) + c - 1
-            if c >= 1 and late >= 0:
-                mask_dh(late)
-            if 1 <= n <= steps:
-                g_mx[n - 1] = quantize("g", g_bf[n - 1][:], 5)
-                if c == 0:
-                    first_product(PAIR * g - 2)
-            if c >= 1 and late >= 0:
-                make_da(late)
-            if 1 <= n <= steps:
-                for u in (2 * n - 2, 2 * n - 1):
-                    w2_mx[u] = quantize("w2", w2_bf[u][:], 8)
-                if c == 0:
-                    first_product(PAIR * g - 1)
-                    w13_mx[g - 1] = quantize("w13", w13_bf[g - 1][:], 2)
-            if c >= 1 and late >= 0:
-                second_product(late)
+            for x in pairs_whose_w13_was_loaded_in(n - 2):
+                round_w13(x)
+
+            if e is not None:
+                mask_dh(e, n)
+            if 1 <= n <= STEPS:
+                g_mx[n - 1] = quantize("g", g_bf[n - 1], 5)
+                first_products_that_are_ready()
+            if e is not None:
+                make_da(e)
+                if e + PAIR < E:
+                    load_saved(e + PAIR)
+            for x in pairs_whose_w13_was_loaded_in(n - 3):
+                w13_mx[x] = quantize("w13", w13_bf[x][:], 2)
+            m = n - W2_QUANT_LAG
+            if 0 <= m < STEPS:
+                w2_mx[m] = quantize("w2", w2_region(m)[:, W2_AT:W2_AT + 2 * TILE_WORDS].bitcast(BF16), 4)
+                first_products_that_are_ready()
+            if e is not None:
+                second_product(e)
 
         halves = 2
-        th = T // halves
-        acc = [None] * halves
-        for r in range(4):
+        width = T // halves
+        total = [None] * halves
+        for r in range(TOP):
             for h in range(halves):
-                picked = dx_sb[:].indirect(pos_sb[r][:, h * th // PER_COL:(h + 1) * th // PER_COL])
-                total = keep.tile([P, th], F32, name="total%d_%d" % (r, h))
+                picked = dx_sb[:].indirect(pos_sb[r][:, h * width // PER_COL:(h + 1) * width // PER_COL])
+                new_total = stage[h][:, r * width:(r + 1) * width]
                 if r == 0:
-                    nc.vector.tensor_copy(total[:], picked)
+                    nc.vector.tensor_copy(new_total, picked)
                 else:
-                    nc.vector.tensor_tensor(total[:], picked, acc[h][:], ALU.add)
-                acc[h] = total
+                    nc.vector.tensor_tensor(new_total, picked, total[h], ALU.add)
+                total[h] = new_total
         for h in range(halves):
-            nc.sync.dma_start(out=out[:, h * th:(h + 1) * th], in_=acc[h][:])
+            nc.sync.dma_start(out=out[:, h * width:(h + 1) * width], in_=total[h])

@@ -90,7 +90,8 @@ def tile_moe_bdx_glu_relu_kernel(
             if u not in w2_raw:
                 w2_raw[u] = ring.tile([P, PACK, H], F32, name="w2_raw", bufs=4)
             rows = w2[e, c * K_PASS:(c + 1) * K_PASS, :].rearrange("(p j) i -> p j i", j=PACK)
-            nc.sync.dma_start(out=w2_raw[u][:, planes, :], in_=rows[:, planes, :])
+            queue = nc.gpsimd if e % PAIR == 1 and e > PAIR and c == 0 else nc.sync
+            queue.dma_start(out=w2_raw[u][:, planes, :], in_=rows[:, planes, :])
 
         def load_w13(g):
             w13_raw[g] = ring.tile([P, 2, PAIR, PACK * K], F32, name="w13_raw", bufs=1)
@@ -263,16 +264,16 @@ def tile_moe_bdx_glu_relu_kernel(
                 second_product(e)
 
         halves = 2
-        width = T // halves
+        tokens = T // halves
         total = [None] * halves
         for r in range(TOP):
             for h in range(halves):
-                picked = dx_sb[:].indirect(pos_sb[r][:, h * width // PER_COL:(h + 1) * width // PER_COL])
-                new_total = stage[h][:, r * width:(r + 1) * width]
+                picked = dx_sb[:].indirect(pos_sb[r][:, h * tokens // PER_COL:(h + 1) * tokens // PER_COL])
+                new_total = stage[h][:, r * tokens:(r + 1) * tokens]
                 if r == 0:
                     nc.vector.tensor_copy(new_total, picked)
                 else:
                     nc.vector.tensor_tensor(new_total, picked, total[h], ALU.add)
                 total[h] = new_total
         for h in range(halves):
-            nc.sync.dma_start(out=out[:, h * width:(h + 1) * width], in_=total[h])
+            nc.sync.dma_start(out=out[:, h * tokens:(h + 1) * tokens], in_=total[h])

from contextlib import ExitStack

import concourse.mybir as mybir

K, T, E, C, H, N = 128, 512, 8, 256, 512, 1536
TOP = 4
S = E * C

P = 128
PACK = 4
K_PASS = P * PACK
PASSES = N // K_PASS
PAIR = 2
PAIRS = E // PAIR
PAIR_SLOTS = PAIR * C
STEPS = PAIRS * PASSES
W2_TILES = E * PASSES
PER_COL = 16
SPARE = 16

TILE_WORDS = PAIR_SLOTS * PACK // 2
STRETCH = PAIR_SLOTS + C
REGION_WORDS = TILE_WORDS + PACK * STRETCH
W2_AT = TILE_WORDS - 16
REGIONS = 4

W2_QUANT_LAG = 2
DA_LAG = 5
DY_LEAD = 4

FLOPS = 2 * S * (N * H + 2 * H * K)
BYTES = 4 * (N * T + 2 * H * S + E * N * H + 2 * E * H * K + S + K * T) + 2 * P * (S + TOP * T) // PER_COL

F32 = mybir.dt.float32
BF16 = mybir.dt.bfloat16
U32 = mybir.dt.uint32
U16 = mybir.dt.uint16
U8 = mybir.dt.uint8
FP8X4 = mybir.dt.float8_e4m3fn_x4
ALU = mybir.AluOpType


def tile_moe_bdx_glu_relu_kernel(
    tc, dyT, a1, a3, w2, w1, w3, gate, offs, pos1, pos2, pos3, pos4, out
):
    nc = tc.nc
    with ExitStack() as ctx:
        keep = ctx.enter_context(tc.tile_pool(name="keep", bufs=1))
        ring = ctx.enter_context(tc.tile_pool(name="ring", bufs=2))
        psum = ctx.enter_context(tc.psum_pool(name="psum", bufs=1))

        offs_sb = keep.tile([P, S // PER_COL], U16, name="offs_sb")
        pos_sb = [keep.tile([P, T // PER_COL], U16, name="pos_sb%d" % r) for r in range(TOP)]
        gate_sb = [keep.tile([P, PAIR_SLOTS], F32, name="gate_sb%d" % g) for g in range(PAIRS)]
        dy_sb = [keep.tile([P, T + SPARE], F32, name="dy_sb%d" % q) for q in range(PASSES * PACK)]
        dx_sb = keep.tile([P, S], F32, name="dx_sb")
        stage = [keep.tile([P, REGION_WORDS], F32, name="stage%d" % r, align_bytes=64) for r in range(REGIONS)]

        w2_raw, w2_mx = {}, {}
        g_raw, g_bf, g_mx = {}, {}, {}
        w13_raw, w13_bf, w13_mx = {}, {}, {}
        saved, dh, dh_masked, da_bf = {}, {}, {}, {}

        def w2_region(n):
            return stage[n % REGIONS]

        def second_use(n):
            return w2_region(n - 1 - W2_QUANT_LAG)

        def stretches(n):
            return second_use(n)[:, TILE_WORDS:REGION_WORDS].rearrange("p (t s) -> p t s", t=PACK)

        def quantize(name, src, bufs):
            width = src.shape[1] // PACK
            codes = ring.tile([P, width], U32, name=name + "_codes", bufs=bufs, align_bytes=64)
            scales = ring.tile([P, width], U8, name=name + "_scales", bufs=bufs, align_bytes=64)
            nc.vector.quantize_mx(out=codes[:].bitcast(FP8X4), scales=scales[:], in_=src)
            return codes, scales

        def load_gate(g):
            nc.sync.dma_start(out=gate_sb[g][:], in_=gate[0:P, g * PAIR_SLOTS:(g + 1) * PAIR_SLOTS])

        def load_dy(q):
            c, t = divmod(q, PACK)
            rows = dyT[c * K_PASS:(c + 1) * K_PASS, :].rearrange("(p t) w -> p t w", t=PACK)
            nc.sync.dma_start(out=dy_sb[q][:, 0:T], in_=rows[:, t, :])

        def load_w2(u, planes=slice(0, PACK)):
            e, c = divmod(u, PASSES)
            if u not in w2_raw:
                w2_raw[u] = ring.tile([P, PACK, H], F32, name="w2_raw", bufs=4)
            rows = w2[e, c * K_PASS:(c + 1) * K_PASS, :].rearrange("(p j) i -> p j i", j=PACK)
            queue = nc.gpsimd if e % PAIR == 1 and e > PAIR and c == 0 else nc.sync
            queue.dma_start(out=w2_raw[u][:, planes, :], in_=rows[:, planes, :])

        def load_w13(g):
            w13_raw[g] = ring.tile([P, 2, PAIR, PACK * K], F32, name="w13_raw", bufs=1)
            for m, w in enumerate((w1, w3)):
                nc.sync.dma_start(
                    out=w13_raw[g][:, m, :, :],
                    in_=w[g * PAIR:(g + 1) * PAIR].rearrange("e (p j) k -> p e (j k)", j=PACK),
                )

        def load_saved(e):
            saved[e] = []
            for m, a in enumerate((a1, a3)):
                a_sb = ring.tile([P, PACK, C], F32, name="a_sb%d_%d" % (m, e % PAIR), bufs=1)
                nc.sync.dma_start(out=a_sb[:], in_=a[:, e * C:(e + 1) * C].rearrange("(p t) s -> p t s", t=PACK))
                saved[e].append(a_sb)

        def gather(n):
            g, c = divmod(n, PASSES)
            g_raw[n] = stretches(n)[:, :, 0:PAIR_SLOTS]
            cols = slice(g * PAIR_SLOTS // PER_COL, (g + 1) * PAIR_SLOTS // PER_COL)
            for t in range(PACK):
                nc.vector.tensor_tensor(
                    g_raw[n][:, t, :], dy_sb[c * PACK + t][:].indirect(offs_sb[:, cols]), gate_sb[g][:], ALU.mult
                )

        def round_g(n):
            if n < STEPS - 1:
                g_bf[n] = second_use(n + 1)[:, 0:TILE_WORDS].bitcast(BF16)
            else:
                g_bf[n] = keep.tile([P, PAIR_SLOTS * PACK], BF16, name="g_last", align_bytes=64)[:]
            nc.scalar.copy(
                out=g_bf[n].rearrange("p (a b t) -> p a t b", b=2, t=PACK),
                in_=g_raw[n].rearrange("p t (a b) -> p a t b", b=2),
            )

        def round_w2(u):
            first = W2_AT + TILE_WORDS * (u % 2)
            rounded = w2_region(u // 2)[:, first:first + TILE_WORDS].bitcast(BF16)
            nc.scalar.copy(
                out=rounded.rearrange("p (th tl m j) -> p th m j tl", th=2, tl=2, j=PACK),
                in_=w2_raw[u][:].rearrange("p j (m th tl) -> p th m j tl", th=2, tl=2),
            )

        def round_w13(g):
            w13_bf[g] = ring.tile([P, 2 * PAIR * K * PACK], BF16, name="w13_bf", bufs=1, align_bytes=64)
            nc.scalar.copy(
                out=w13_bf[g][:].rearrange("p (x a b j) -> p x a j b", b=2, j=PACK, x=2 * PAIR),
                in_=w13_raw[g][:].rearrange("p m e (j a b) -> p (m e) a j b", b=2, j=PACK),
            )

        def first_product(e):
            g, half = divmod(e, PAIR)
            slots = slice(half * C, (half + 1) * C)
            dh[e] = [psum.tile([P, 2, C], F32, name="dh%d" % b, bufs=3) for b in range(2)]
            for t in (0, 2, 1, 3):
                for c in range(PASSES):
                    step, second = divmod(e * PASSES + c, 2)
                    w_codes, w_scales = w2_mx[step]
                    cols = slice(second * H + t * P, second * H + (t + 1) * P)
                    g_codes, g_scales = g_mx[g * PASSES + c]
                    nc.tensor.matmul_mx(
                        out=dh[e][t % 2][:, t // 2, :],
                        lhsT=w_codes[:, cols].bitcast(FP8X4), lhsT_scale=w_scales[:, cols],
                        rhs=g_codes[:, slots].bitcast(FP8X4), rhs_scale=g_scales[:, slots],
                        start=(c == 0), stop=(c == PASSES - 1),
                    )

        def first_products_that_are_ready():
            for e in range(E):
                last_w2_step = (e * PASSES + PASSES - 1) // 2
                last_g_step = (e // PAIR) * PASSES + PASSES - 1
                if e not in dh and last_w2_step in w2_mx and last_g_step in g_mx:
                    first_product(e)

        def mask_dh(e, n):
            dh_masked[e] = stretches(n)[:, :, PAIR_SLOTS:STRETCH]
            for b in range(2):
                nc.vector.scalar_tensor_tensor(
                    out=dh_masked[e][:, b:PACK:2, :], in0=saved[e][0][:, b:PACK:2, :], scalar=0.0,
                    in1=dh[e][b][:], op0=ALU.is_gt, op1=ALU.mult,
                )

        def make_da(e):
            da_bf[e] = []
            for m in range(2):
                da = ring.tile([P, C * PACK], BF16, name="da_bf%d" % m, bufs=2, align_bytes=64)
                nc.vector.tensor_tensor(
                    da[:].rearrange("p (a b t) -> p a t b", b=2, t=PACK),
                    dh_masked[e].rearrange("p t (a b) -> p a t b", b=2),
                    saved[e][1 - m][:].rearrange("p t (a b) -> p a t b", b=2),
                    ALU.mult,
                )
                da_bf[e].append(da)

        def second_product(e):
            g, half = divmod(e, PAIR)
            da_mx = [quantize("da%d" % m, da_bf[e][m][:], 2) for m in range(2)]
            dx_ps = psum.tile([P, C], F32, name="dx_ps", bufs=2)
            w_codes, w_scales = w13_mx[g]
            for m in range(2):
                cols = slice((m * PAIR + half) * K, (m * PAIR + half + 1) * K)
                nc.tensor.matmul_mx(
                    out=dx_ps[:],
                    lhsT=w_codes[:, cols].bitcast(FP8X4), lhsT_scale=w_scales[:, cols],
                    rhs=da_mx[m][0][:].bitcast(FP8X4), rhs_scale=da_mx[m][1][:],
                    start=(m == 0), stop=(m == 1),
                )
            nc.scalar.copy(out=dx_sb[:, e * C:(e + 1) * C], in_=dx_ps[:])

        def pairs_whose_w13_was_loaded_in(n):
            return [g for g in range(PAIRS) if n == PASSES * max(g - 1, 0)]

        expert_of_step = {PASSES * (e // PAIR) + e % PAIR + DA_LAG: e for e in range(E)}

        for q in range(PASSES * PACK):
            nc.gpsimd.memset(dy_sb[q][:, T:T + SPARE], 0.0)
        nc.sync.dma_start(out=offs_sb[:], in_=offs)
        load_gate(0)
        for i in range(PASSES * PACK + DY_LEAD):
            if i < PASSES * PACK:
                load_dy(i)
            if i >= DY_LEAD:
                u, j = divmod(i - DY_LEAD, PACK)
                load_w2(u, slice(j, j + 1))

        for n in range(max(expert_of_step) + 1):
            g, c = divmod(n, PASSES)
            e = expert_of_step.get(n)

            if c == 0 and g + 1 < PAIRS:
                load_gate(g + 1)
            for u in (PASSES + 2 * n, PASSES + 2 * n + 1):
                if u < W2_TILES:
                    load_w2(u)
            for x in pairs_whose_w13_was_loaded_in(n):
                load_w13(x)
            if 1 <= n <= PAIR:
                load_saved(n - 1)
            if n == STEPS - PASSES:
                for r, pos in enumerate((pos1, pos2, pos3, pos4)):
                    nc.sync.dma_start(out=pos_sb[r][:], in_=pos)

            if n < STEPS:
                gather(n)
                if n >= 1:
                    round_g(n - 1)
                if n == STEPS - 1:
                    round_g(n)
                round_w2(2 * n)
                round_w2(2 * n + 1)
            for x in pairs_whose_w13_was_loaded_in(n - 2):
                round_w13(x)

            if e is not None:
                mask_dh(e, n)
            if 1 <= n <= STEPS:
                g_mx[n - 1] = quantize("g", g_bf[n - 1], 5)
                first_products_that_are_ready()
            if e is not None:
                make_da(e)
                if e + PAIR < E:
                    load_saved(e + PAIR)
            for x in pairs_whose_w13_was_loaded_in(n - 3):
                w13_mx[x] = quantize("w13", w13_bf[x][:], 2)
            m = n - W2_QUANT_LAG
            if 0 <= m < STEPS:
                w2_mx[m] = quantize("w2", w2_region(m)[:, W2_AT:W2_AT + 2 * TILE_WORDS].bitcast(BF16), 4)
                first_products_that_are_ready()
            if e is not None:
                second_product(e)

        halves = 2
        tokens = T // halves
        total = [None] * halves
        for r in range(TOP):
            for h in range(halves):
                picked = dx_sb[:].indirect(pos_sb[r][:, h * tokens // PER_COL:(h + 1) * tokens // PER_COL])
                new_total = stage[h][:, r * tokens:(r + 1) * tokens]
                if r == 0:
                    nc.vector.tensor_copy(new_total, picked)
                else:
                    nc.vector.tensor_tensor(new_total, picked, total[h], ALU.add)
                total[h] = new_total
        for h in range(halves):
            nc.sync.dma_start(out=out[:, h * tokens:(h + 1) * tokens], in_=total[h])
